import numpy as np
import ml_dtypes


def mxq(x, axis, fmt="e4m3"):
    dtype, down = {"e4m3": (ml_dtypes.float8_e4m3fn, 7), "e5m2": (ml_dtypes.float8_e5m2, 14)}[fmt]
    v = np.moveaxis(np.asarray(x, np.float32).astype(ml_dtypes.bfloat16).astype(np.float64), axis, -1)
    blocks = v.reshape(v.shape[:-1] + (-1, 32))
    amax = np.abs(blocks).max(-1, keepdims=True)
    byte = np.maximum(np.where(amax > 0, np.frexp(amax)[1] - 1 + 127, 0) - down, 1)
    scale = np.exp2(byte - 127.0)
    codes = (blocks / scale).astype(np.float32).astype(dtype).astype(np.float64)
    return np.moveaxis((codes * scale).reshape(v.shape), -1, axis)


WIDE = False


def mx_kscale(k):
    if not WIDE:
        return np.ones(k)
    levels = np.array([10, -10, 5, -5, 0])
    if k % 512:
        return np.exp2(np.random.permutation(np.resize(levels, k // 32))).repeat(32)
    a = np.empty((k // 512, 16))
    for p in range(k // 512):
        a[p, :8] = np.random.permutation(np.resize(levels, 8))
        for g in range(8):
            far = levels[np.abs(levels - a[p, g]) >= 10]
            a[p, g + 8] = far[np.random.randint(len(far))]
    return np.exp2(a.ravel()).repeat(32)


def f64(x):
    return np.asarray(x).astype(np.float64)


def striped(idx):
    return np.tile(idx.reshape(-1, 16).T, (8, 1)).astype(np.uint16)


def unstriped(offs):
    return offs[:16].T.reshape(-1).astype(np.int64)


E2M1 = np.array([0.0, 0.5, 1.0, 1.5, 2.0, 3.0, 4.0, 6.0, -0.0, -0.5, -1.0, -1.5, -2.0, -3.0, -4.0, -6.0])


def pack_weight(w, fmt):
    k, n = w.shape
    w = f64(np.asarray(w, np.float32).astype(ml_dtypes.bfloat16)).reshape(k // 32, 32, n)
    amax = np.abs(w).max(1)
    if fmt == "e4m3":
        byte = np.frexp(amax)[1] - 1 + 127 - 7
    else:
        mant, ex = np.frexp(amax / 6.0)
        byte = np.where(mant > 0.5, ex, ex - 1) + 127
    byte = np.clip(np.where(amax > 0, byte, 1), 1, 254)
    scaled = (w * np.exp2(127.0 - byte)[:, None, :]).reshape(k, n).astype(np.float32)
    by_word = np.ascontiguousarray(scaled.reshape(k // 512, 128, 4, n).transpose(0, 1, 3, 2))
    if fmt == "e4m3":
        words = by_word.astype(ml_dtypes.float8_e4m3fn).view(np.uint8)
    else:
        c = by_word.astype(ml_dtypes.float4_e2m1fn).view(np.uint8) & 0xF
        words = (c[..., 0::2] | (c[..., 1::2] << 4)).reshape(k // 512, 128, 2 * n)
    return np.ascontiguousarray(words), np.ascontiguousarray(byte.astype(np.uint8).reshape(k // 512, 16, n))


def unpack_weight(words, scales, fmt):
    g, _, n = scales.shape
    words = np.ascontiguousarray(words).reshape(g, 128, n, -1)
    if fmt == "e4m3":
        vals = words.view(ml_dtypes.float8_e4m3fn).astype(np.float64)
    else:
        nib = np.empty((g, 128, n, 4), np.uint8)
        nib[..., 0::2] = words & 0xF
        nib[..., 1::2] = words >> 4
        vals = E2M1[nib]
    vals = vals * np.repeat(np.exp2(scales.astype(np.float64) - 127.0), 8, axis=1)[..., None]
    return vals.transpose(0, 1, 3, 2).reshape(g * 512, n)


def gelu(v):
    return 0.5 * v * (1.0 + np.tanh(np.sqrt(2.0 / np.pi) * (v + 0.044715 * v**3)))


K, R, H, N, T, S, T2, P = 1024, 512, 512, 512, 4096, 1024, 2048, 512

def setup_inputs():
    n = np.random.standard_normal
    s = mx_kscale(K)[:, None]
    u1 = mx_kscale(R)[:, None]
    u = mx_kscale(H)[:, None]
    tab_words, tab_scales = pack_weight(n((K, T)) * s, "e4m3")
    w2_words, w2_scales = pack_weight(1.25 * n((R, H)) / np.sqrt(R) / u1 * u.T, "e2m1")
    perm = np.random.permutation(T2)
    return {
        "tab_words": tab_words, "tab_scales": tab_scales,
        "offs": striped(np.random.permutation(T)[:S]),
        "w1": (1.5 * n((K, R)) / np.sqrt(K) / s).astype(np.float32),
        "gain": (np.exp(0.3 * n(R)) * u1[:, 0]).astype(np.float32),
        "w2_words": w2_words, "w2_scales": w2_scales,
        "w3": (n((K, H)) / np.sqrt(K) / s * u.T).astype(np.float32),
        "page0": (n((H, T2)) * u).astype(np.float32),
        "wgs": np.exp(0.3 * n((128, S))).astype(np.float32),
        "offs2": striped(np.random.permutation(T2)[:S]),
        "offs3": striped(perm[:P]),
        "offs4": striped(perm[P:2 * P]),
        "mirror": (1.4 * np.exp(0.5 * n(H)) / u[:, 0]).astype(np.float32),
        "w4": (n((H, N)) / np.sqrt(H) / u).astype(np.float32),
    }

def reference(tab_words, tab_scales, offs, w1, gain, w2_words, w2_scales, w3, page0, wgs, offs2, offs3, offs4, mirror, w4):
    v = unpack_weight(tab_words, tab_scales, "e4m3")[:, unstriped(offs)]
    w2 = unpack_weight(w2_words, w2_scales, "e2m1")
    d = np.tanh(mxq(f64(w1), 0, "e4m3").T @ v) * f64(gain)[:, None]
    deep = w2.T @ mxq(d, 0, "e4m3")
    direct = mxq(f64(w3), 0, "e4m3").T @ v
    h = np.maximum(deep, direct)
    page = f64(page0).copy()
    page[:, unstriped(offs2)] = np.tile(f64(wgs), (H // 128, 1)) * h
    a = page[:, unstriped(offs3)]
    b = page[:, unstriped(offs4)]
    page[:, unstriped(offs3)] = a * np.tanh(f64(mirror)[:, None] * b)
    page[:, unstriped(offs4)] = a + b
    return mxq(f64(w4), 0, "e4m3").T @ mxq(page, 0, "e4m3")

@@ -1,0 +1,332 @@
+from contextlib import ExitStack
+
+import concourse.mybir as mybir
+
+K, R, H, N, T, S, T2, PAIRS = 1024, 512, 512, 512, 4096, 1024, 2048, 512
+FLOPS = 2 * S * (K * R + R * H + K * H) + 2 * H * N * T2
+
+F32 = mybir.dt.float32
+BF16 = mybir.dt.bfloat16
+I32 = mybir.dt.int32
+U32 = mybir.dt.uint32
+U16 = mybir.dt.uint16
+U8 = mybir.dt.uint8
+FP8X4 = mybir.dt.float8_e4m3fn_x4
+FP4X4 = mybir.dt.float4_e2m1fn_x4
+ALU = mybir.AluOpType
+ACT = mybir.ActivationFunctionType
+
+P = 128
+PACK = 4
+BANK = 512
+HALF = S // 2
+PER_COLUMN = 16
+TILE_ORDER = (0, 2, 3, 1)
+OUT_WIDTHS = (256, 256, 512, 512, 512)
+
+
+def tile_list_scouting_belief_exchange_kernel(
+    tc, tab_words, tab_scales, offs, w1, gain, w2_words, w2_scales, w3, page0, wgs, offs2, offs3, offs4, mirror, w4, out
+):
+    nc = tc.nc
+    with ExitStack() as ctx:
+        sb = ctx.enter_context(tc.tile_pool(name="sb", bufs=1))
+        ps = ctx.enter_context(tc.psum_pool(name="ps", bufs=1))
+
+        def sbuf(shape, dtype, name, tag=None):
+            return sb.tile(shape, dtype, name=name, tag=tag or name, align_bytes=64)
+
+        banks = [ps.tile([P, BANK], F32, name="bank%d" % i) for i in range(8)]
+
+        idx = sbuf([P, S // PER_COLUMN], U16, "idx")
+        idx2 = sbuf([P, S // PER_COLUMN], U16, "idx2")
+        idx3 = sbuf([P, PAIRS // PER_COLUMN], U16, "idx3")
+        idx4 = sbuf([P, PAIRS // PER_COLUMN], U16, "idx4")
+        table = [sbuf([P, T], U32, "table%d" % a) for a in range(2)]
+        table_scales = sbuf([P, T], U8, "table_scales")
+        w1_raw = [sbuf([P, PACK, R], F32, "w1_raw%d" % a, "raw%d" % a) for a in range(2)]
+        w3_raw = [sbuf([P, PACK, H], F32, "w3_raw%d" % a, "raw%d" % (2 + a)) for a in range(2)]
+        w2_raw = sbuf([P, 2 * H], U8, "w2_raw")
+        w2_raw_scales = sbuf([P, H], U8, "w2_raw_scales")
+        gains = sbuf([P, 1, PACK], F32, "gains")
+        mirrors = sbuf([P, PACK], F32, "mirrors")
+        page = [sbuf([P, T2], F32, "page%d" % t) for t in range(PACK)]
+        weights = [sbuf([P, S], F32, "wgs%d" % t) for t in range(PACK)]
+
+        nc.gpsimd.memset(w2_raw_scales[:].bitcast(I32), 0)
+        nc.gpsimd.memset(table_scales[:, : 3 * T // 4].bitcast(I32), 0)
+        nc.vector.memset(table_scales[:, 3 * T // 4 :].bitcast(I32), 0)
+
+        def load_rows(tile, w, a):
+            nc.sync.dma_start(tile[:], w[512 * a : 512 * (a + 1), :].rearrange("(p j) c -> p j c", j=PACK))
+
+        def load_table(a):
+            nc.sync.dma_start(table[a][:].bitcast(I32), tab_words[a].rearrange("p t i -> p (t i)").bitcast(I32))
+
+        def load_page(t):
+            nc.sync.dma_start(page[t][:], page0.rearrange("(p t) c -> t p c", t=PACK)[t])
+            for q in range(4):
+                nc.sync.dma_start(weights[t][32 * q : 32 * (q + 1), :], wgs.rearrange("(u t) j -> t u j", t=PACK)[t])
+
+        for a in range(2):
+            load_rows(w1_raw[a], w1, a)
+            for q in range(4):
+                nc.sync.dma_start(
+                    table_scales[32 * q + 4 * a : 32 * q + 4 * a + 4, :].bitcast(I32),
+                    tab_scales[a, 4 * q : 4 * q + 4, :].bitcast(I32),
+                )
+        nc.sync.dma_start(idx[:], offs)
+        load_table(0)
+        nc.sync.dma_start(w2_raw[:].bitcast(I32), w2_words[0].bitcast(I32))
+        for q in range(4):
+            nc.sync.dma_start(
+                w2_raw_scales[32 * q : 32 * q + 4, :].bitcast(I32), w2_scales[0, 4 * q : 4 * q + 4, :].bitcast(I32)
+            )
+        load_table(1)
+        load_rows(w3_raw[0], w3, 0)
+        nc.sync.dma_start(gains[:, 0, :], gain.rearrange("(p t) -> p t", t=PACK))
+        nc.sync.dma_start(idx2[:], offs2)
+        load_rows(w3_raw[1], w3, 1)
+        load_page(TILE_ORDER[0])
+        load_page(TILE_ORDER[1])
+        load_page(TILE_ORDER[2])
+        load_page(TILE_ORDER[3])
+        nc.sync.dma_start(idx3[:], offs3)
+        nc.sync.dma_start(idx4[:], offs4)
+        nc.sync.dma_start(mirrors[:], mirror.rearrange("(p t) -> p t", t=PACK))
+        w4_raw = sbuf([P, PACK, N], F32, "w4_raw", "raw0")
+        load_rows(w4_raw, w4, 0)
+
+        w1_codes = [sbuf([P, R], U32, "w1_codes%d" % a) for a in range(2)]
+        w1_scales = [sbuf([P, R], U8, "w1_scales%d" % a) for a in range(2)]
+        w3_codes = [sbuf([P, H], U32, "w3_codes%d" % a) for a in range(2)]
+        w3_scales = [sbuf([P, H], U8, "w3_scales%d" % a) for a in range(2)]
+
+        def deal(copy, raw, t0, nt, name, tag):
+            dealt = sbuf([P, nt, P, PACK], BF16, name, tag)
+            copy(
+                dealt[:].rearrange("p t m j -> p m j t"),
+                raw[:].rearrange("p j (m t) -> p m j t", t=PACK)[:, :, :, t0 : t0 + nt],
+            )
+            return dealt
+
+        def quantise_dealt(dealt, codes, scales, t0, nt):
+            cols = slice(P * t0, P * (t0 + nt))
+            nc.vector.quantize_mx(codes[:, cols].bitcast(FP8X4), scales[:, cols], dealt[:].rearrange("p t m j -> p (t m j)"))
+
+        for a in range(2):
+            quantise_dealt(deal(nc.vector.tensor_copy, w1_raw[a], 0, PACK, "w1_dealt%d" % a, "wide%d" % a),
+                           w1_codes[a], w1_scales[a], 0, PACK)
+
+
+        v_codes = [sbuf([P, S], U32, "v_codes%d" % a) for a in range(2)]
+        v_scales = sbuf([P, S], U8, "v_scales")
+
+        def entries(tile, j0, n):
+            return tile[:, j0 // PER_COLUMN : (j0 + n) // PER_COLUMN]
+
+        def gather_words(a, j0, n):
+            nc.vector.tensor_copy(v_codes[a][:, j0 : j0 + n], table[a][:].indirect(entries(idx, j0, n)))
+
+        def times_v(acc, codes, scales, t, a, j0, n, start, stop):
+            cols = slice(P * t, P * (t + 1))
+            nc.tensor.matmul_mx(
+                acc, lhsT=codes[a][:, cols].bitcast(FP8X4), lhsT_scale=scales[a][:, cols],
+                rhs=v_codes[a][:, j0 : j0 + n].bitcast(FP8X4), rhs_scale=v_scales[4 * a :, j0 : j0 + n],
+                start=start, stop=stop,
+            )
+
+        nc.vector.tensor_copy(v_scales[:], table_scales[:].indirect(idx[:]))
+        gather_words(0, 0, S)
+
+        w2_codes = sbuf([P, 2 * H], U8, "w2_codes")
+        w2_dealt_scales = sbuf([P, H], U8, "w2_dealt_scales")
+        nc.vector.tensor_copy(
+            w2_codes[:].rearrange("p (t m b) -> p m t b", t=PACK, b=2),
+            w2_raw[:].rearrange("p (m t b) -> p m t b", t=PACK, b=2),
+        )
+        nc.vector.tensor_copy(
+            w2_dealt_scales[:].rearrange("p (t m) -> p m t", t=PACK),
+            w2_raw_scales[:].rearrange("p (m t) -> p m t", t=PACK),
+        )
+
+        d_codes = sbuf([P, S], U32, "d_codes")
+        d_scales = sbuf([P, S], U8, "d_scales")
+
+        def quantise_d(rounded, j0, n):
+            nc.vector.quantize_mx(d_codes[:, j0 : j0 + n].bitcast(FP8X4), d_scales[:, j0 : j0 + n],
+                                  rounded[:].rearrange("p j t -> p (j t)"))
+
+        def first_half_pass(s, a):
+            for t in range(PACK):
+                times_v(banks[s][:, P * t : P * (t + 1)], w1_codes, w1_scales, t, a, P * s, P,
+                        a == 0 and t == 0, a == 1 and t == PACK - 1)
+
+        def first_half_tanh(s):
+            bent = sbuf([P, P, PACK], F32, "bent%d" % s, "bent%d" % s)
+            nc.scalar.activation(bent[:], banks[s][:].rearrange("p (t j) -> p j t", t=PACK), ACT.Tanh)
+            return bent
+
+        def first_half_gain(rounded, s, bent):
+            nc.vector.tensor_tensor(rounded[:, P * (s % 2) : P * (s % 2 + 1), :], bent[:],
+                                    gains[:].to_broadcast([P, P, PACK]), ALU.mult)
+
+        direct_sb = [sbuf([P, HALF], F32, "direct%d" % i) for i in range(3)]
+        h_sb = [sbuf([P, HALF], F32, "h%d" % i) for i in range(4)]
+        a_t, b_t, c_t, d_t = TILE_ORDER
+        units = [(a_t, 0, 256), (a_t, 256, 256), (b_t, 0, HALF), (c_t, 0, HALF), (d_t, 0, HALF),
+                 (a_t, HALF, HALF), (b_t, HALF, HALF), (c_t, HALF, HALF), (d_t, HALF, HALF)]
+
+        def make_h(k):
+            t, j0, n = units[k]
+            direct_bank, deep_bank = banks[4 + 2 * (k % 2)], banks[5 + 2 * (k % 2)]
+            for a in range(2):
+                times_v(direct_bank[:, :n], w3_codes, w3_scales, t, a, j0, n, a == 0, a == 1)
+            nc.scalar.copy(direct_sb[k % 3][:, :n], direct_bank[:, :n])
+            nc.tensor.matmul_mx(
+                deep_bank[:, :n], lhsT=w2_codes[:, 2 * P * t : 2 * P * (t + 1)].bitcast(FP4X4),
+                lhsT_scale=w2_dealt_scales[:, P * t : P * (t + 1)],
+                rhs=d_codes[:, j0 : j0 + n].bitcast(FP8X4), rhs_scale=d_scales[:, j0 : j0 + n], start=True, stop=True,
+            )
+            nc.vector.tensor_tensor(h_sb[k % 4][:, :n], deep_bank[:, :n], direct_sb[k % 3][:, :n], ALU.max)
+
+        def put_h(k):
+            t, j0, n = units[k]
+            nc.vector.tensor_tensor(page[t][:].indirect(entries(idx2, j0, n)), h_sb[k % 4][:, :n],
+                                    weights[t][:, j0 : j0 + n], ALU.mult)
+
+        for s in range(4):
+            first_half_pass(s, 0)
+        gather_words(1, 0, 256)
+        first_half_pass(0, 1)
+        first_half_pass(1, 1)
+        bent = [first_half_tanh(0), first_half_tanh(1)]
+        gather_words(1, 256, 256)
+        first_half_pass(2, 1)
+        first_half_pass(3, 1)
+        bent = bent + [first_half_tanh(2), first_half_tanh(3)]
+        d_rounded = [sbuf([P, 256, PACK], BF16, "d_rounded%d" % c) for c in range(2)]
+        first_half_gain(d_rounded[0], 0, bent[0])
+        first_half_gain(d_rounded[0], 1, bent[1])
+        low0 = deal(nc.vector.tensor_copy, w3_raw[0], 0, 2, "w3_low0", "narrow0")
+        quantise_d(d_rounded[0], 0, 256)
+        first_half_gain(d_rounded[1], 2, bent[2])
+        quantise_dealt(low0, w3_codes[0], w3_scales[0], 0, 2)
+        high0 = deal(nc.scalar.copy, w3_raw[0], 2, 2, "w3_high0", "narrow2")
+        first_half_gain(d_rounded[1], 3, bent[3])
+        low1 = deal(nc.vector.tensor_copy, w3_raw[1], 0, 2, "w3_low1", "narrow1")
+        quantise_d(d_rounded[1], 256, 256)
+        quantise_dealt(low1, w3_codes[1], w3_scales[1], 0, 2)
+        high1 = deal(nc.scalar.copy, w3_raw[1], 2, 2, "w3_high1", "narrow3")
+        gather_words(1, HALF, HALF)
+        make_h(0)
+        make_h(1)
+        quantise_dealt(high0, w3_codes[0], w3_scales[0], 2, 2)
+        put_h(0)
+        quantise_dealt(high1, w3_codes[1], w3_scales[1], 2, 2)
+        put_h(1)
+        make_h(2)
+        make_h(3)
+
+        scaled = sbuf([P, PACK, HALF], BF16, "d_scaled", "wide2")
+        for t in range(PACK):
+            for a in range(2):
+                times_v(banks[t][:], w1_codes, w1_scales, t, a, HALF, HALF, a == 0, a == 1)
+            late = sbuf([P, HALF], F32, "late%d" % t, "bent%d" % t)
+            nc.scalar.activation(late[:], banks[t][:], ACT.Tanh)
+            nc.scalar.activation(scaled[:, t, :], late[:], ACT.Copy, scale=gains[:, 0, t : t + 1])
+        d_late = sbuf([P, HALF, PACK], BF16, "d_late")
+        put_h(2)
+        make_h(4)
+        nc.scalar.copy(d_late[:].rearrange("p (c i) t -> p c t i", i=4), scaled[:].rearrange("p t (c i) -> p c t i", i=4))
+        put_h(3)
+        quantise_d(d_late, HALF, HALF)
+        make_h(5)
+        put_h(4)
+        make_h(6)
+        put_h(5)
+        make_h(7)
+        put_h(6)
+
+        w4_rounded = sbuf([P, N, PACK], BF16, "w4_rounded", "wide0")
+        w4_codes = sbuf([P, N], U32, "w4_codes")
+        w4_scales = sbuf([P, N], U8, "w4_scales")
+
+        one_side = [sbuf([P, PAIRS], F32, "one_side%d" % i) for i in range(2)]
+        other_side = [sbuf([P, PAIRS], F32, "other_side%d" % i) for i in range(2)]
+        gate = [sbuf([P, PAIRS], F32, "gate%d" % i) for i in range(2)]
+
+        def fetch(i):
+            t = TILE_ORDER[i]
+            nc.vector.tensor_copy(other_side[i % 2][:], page[t][:].indirect(idx4[:]))
+            nc.vector.tensor_copy(one_side[i % 2][:], page[t][:].indirect(idx3[:]))
+            nc.scalar.activation(gate[i % 2][:], other_side[i % 2][:], ACT.Tanh, scale=mirrors[:, t : t + 1])
+
+        def put_sum(i):
+            nc.vector.tensor_tensor(page[TILE_ORDER[i]][:].indirect(idx4[:]), one_side[i % 2][:], other_side[i % 2][:], ALU.add)
+
+        def put_gated(i):
+            nc.vector.tensor_tensor(page[TILE_ORDER[i]][:].indirect(idx3[:]), one_side[i % 2][:], gate[i % 2][:], ALU.mult)
+
+        starts = [sum(OUT_WIDTHS[:c]) for c in range(len(OUT_WIDTHS))]
+        tags = ("narrow0", "narrow1", "wide1", "wide2", "d_late")
+        rounded = [sbuf([P, w, PACK], BF16, "page_rounded%d" % c, tags[c]) for c, w in enumerate(OUT_WIDTHS)]
+
+        def round_page(copy, t, c):
+            copy(rounded[c][:, :, t], page[t][:, starts[c] : starts[c] + OUT_WIDTHS[c]])
+
+        def round_early(i):
+            for c in range(len(OUT_WIDTHS)):
+                round_page(nc.scalar.copy, TILE_ORDER[i], c)
+
+        fetch(0)
+        make_h(8)
+        nc.scalar.copy(w4_rounded[:].rearrange("p (c i) j -> p c j i", i=4), w4_raw[:].rearrange("p j (c i) -> p c j i", i=4))
+        put_h(7)
+        put_sum(0)
+        fetch(1)
+        put_gated(0)
+        round_early(0)
+        put_sum(1)
+        fetch(2)
+        put_gated(1)
+        round_early(1)
+        put_h(8)
+        put_sum(2)
+        fetch(3)
+        put_gated(2)
+        round_early(2)
+        put_sum(3)
+        nc.vector.quantize_mx(w4_codes[:].bitcast(FP8X4), w4_scales[:], w4_rounded[:].rearrange("p n j -> p (n j)"))
+        put_gated(3)
+
+        page_codes = [sbuf([P, w], U32, "page_codes%d" % c) for c, w in enumerate(OUT_WIDTHS)]
+        page_scales = [sbuf([P, w], U8, "page_scales%d" % c) for c, w in enumerate(OUT_WIDTHS)]
+        stage_tags = ("stage", "raw1", "raw2", "raw3", "raw0")
+        first_bank = (0, 2, 4, 0, 4)
+        out_rows = out.rearrange("(g p) c -> p g c", p=P)
+
+        def finish(c):
+            w = OUT_WIDTHS[c]
+            per_bank = BANK // w
+            nc.vector.quantize_mx(page_codes[c][:].bitcast(FP8X4), page_scales[c][:], rounded[c][:].rearrange("p c t -> p (c t)"))
+            stage = sbuf([P, PACK, w], F32, "stage%d" % c, stage_tags[c])
+            for g in range(PACK):
+                bank = banks[first_bank[c] + g // per_bank]
+                nc.tensor.matmul_mx(
+                    bank[:, w * (g % per_bank) : w * (g % per_bank + 1)],
+                    lhsT=w4_codes[:, P * g : P * (g + 1)].bitcast(FP8X4), lhsT_scale=w4_scales[:, P * g : P * (g + 1)],
+                    rhs=page_codes[c][:].bitcast(FP8X4), rhs_scale=page_scales[c][:], start=True, stop=True,
+                )
+                if g % per_bank == per_bank - 1:
+                    copy = nc.vector.tensor_copy if (per_bank == 1 and g == PACK - 1) else nc.scalar.copy
+                    g0 = g - per_bank + 1
+                    copy(stage[:, g0 : g + 1, :].rearrange("p g c -> p (g c)"), bank[:])
+                if g % 2 == 1:
+                    nc.sync.dma_start(out_rows[:, g - 1 : g + 1, starts[c] : starts[c] + w], stage[:, g - 1 : g + 1, :])
+
+        round_page(nc.vector.tensor_copy, d_t, 0)
+        for c in range(len(OUT_WIDTHS)):
+            if c + 1 < len(OUT_WIDTHS):
+                round_page(nc.vector.tensor_copy, d_t, c + 1)
+            finish(c)

@@ -20,6 +20,7 @@ P = 128
 PACK = 4
 BANK = 512
 HALF = S // 2
+QUARTER = S // 4
 PER_COLUMN = 16
 TILE_ORDER = (0, 2, 3, 1)
 OUT_WIDTHS = (256, 256, 512, 512, 512)
@@ -51,11 +52,21 @@ def tile_list_scouting_belief_exchange_kernel(
         gains = sbuf([P, 1, PACK], F32, "gains")
         mirrors = sbuf([P, PACK], F32, "mirrors")
         page = [sbuf([P, T2], F32, "page%d" % t) for t in range(PACK)]
-        weights = [sbuf([P, S], F32, "wgs%d" % t) for t in range(PACK)]
+        a_t, b_t, c_t, d_t = TILE_ORDER
+        early_a = [sbuf([P, 1, QUARTER], F32, "wgs_early_a%d" % c) for c in range(2)]
+        early_bc = sbuf([P, 2, HALF], F32, "wgs_early_bc")
+        early_d = sbuf([P, 1, HALF], F32, "wgs_early_d")
+        late_ad = sbuf([P, 2, HALF], F32, "wgs_late_ad")
+        late_bc = sbuf([P, 2, HALF], F32, "wgs_late_bc")
+        late_weights = {a_t: late_ad[:, 0, :], d_t: late_ad[:, 1, :], b_t: late_bc[:, 0, :], c_t: late_bc[:, 1, :]}
+        early_weights = {b_t: early_bc[:, 0, :], c_t: early_bc[:, 1, :], d_t: early_d[:, 0, :]}
 
         nc.gpsimd.memset(w2_raw_scales[:].bitcast(I32), 0)
-        nc.gpsimd.memset(table_scales[:, : 3 * T // 4].bitcast(I32), 0)
-        nc.vector.memset(table_scales[:, 3 * T // 4 :].bitcast(I32), 0)
+        nc.gpsimd.memset(table_scales[32:64, :].bitcast(I32), 0)
+        nc.vector.memset(table_scales[64:, :].bitcast(I32), 0)
+        v_scales = [sbuf([P, S], U8, "v_scales%d" % a) for a in range(2)]
+        for a in range(2):
+            nc.vector.memset(v_scales[a][:].bitcast(I32), 0)
 
         def load_rows(tile, w, a):
             nc.sync.dma_start(tile[:], w[512 * a : 512 * (a + 1), :].rearrange("(p j) c -> p j c", j=PACK))
@@ -65,44 +76,60 @@ def tile_list_scouting_belief_exchange_kernel(
 
         def load_page(t):
             nc.sync.dma_start(page[t][:], page0.rearrange("(p t) c -> t p c", t=PACK)[t])
-            for q in range(4):
-                nc.sync.dma_start(weights[t][32 * q : 32 * (q + 1), :], wgs.rearrange("(u t) j -> t u j", t=PACK)[t])
 
-        for a in range(2):
-            load_rows(w1_raw[a], w1, a)
-            for q in range(4):
-                nc.sync.dma_start(
-                    table_scales[32 * q + 4 * a : 32 * q + 4 * a + 4, :].bitcast(I32),
-                    tab_scales[a, 4 * q : 4 * q + 4, :].bitcast(I32),
-                )
+        def load_weights(tile, t0, nt, j0, n=HALF):
+            rows = wgs.rearrange("(u t) j -> u t j", t=PACK)[:, t0 : t0 + nt, j0 : j0 + n]
+            for q in (0, 2, 1, 3):
+                nc.sync.dma_start(tile[32 * q : 32 * (q + 1), :, :], rows)
+
+        def entries(tile, j0, n):
+            return tile[:, j0 // PER_COLUMN : (j0 + n) // PER_COLUMN]
+
+        picked_scales = sbuf([P, S], U8, "picked_scales")
+
+        def place_scales(a, r):
+            nc.sync.dma_start(
+                v_scales[a][r:P:32, :].bitcast(I32), picked_scales[16 * a + r : 16 * (a + 1) : 4, :].bitcast(I32)
+            )
+
+        nc.sync.dma_start(table_scales[:32, :].bitcast(I32), tab_scales.rearrange("a q t -> (a q) t").bitcast(I32))
         nc.sync.dma_start(idx[:], offs)
-        load_table(0)
+        load_rows(w1_raw[0], w1, 0)
         nc.sync.dma_start(w2_raw[:].bitcast(I32), w2_words[0].bitcast(I32))
         for q in range(4):
             nc.sync.dma_start(
                 w2_raw_scales[32 * q : 32 * q + 4, :].bitcast(I32), w2_scales[0, 4 * q : 4 * q + 4, :].bitcast(I32)
             )
+        load_rows(w1_raw[1], w1, 1)
+        load_table(0)
+        nc.vector.tensor_copy(picked_scales[:], table_scales[:].indirect(idx[:]))
+        scale_rows = [(a, r) for a in range(2) for r in range(4)]
+        for a, r in scale_rows[:6]:
+            place_scales(a, r)
         load_table(1)
+        for a, r in scale_rows[6:]:
+            place_scales(a, r)
         load_rows(w3_raw[0], w3, 0)
         nc.sync.dma_start(gains[:, 0, :], gain.rearrange("(p t) -> p t", t=PACK))
         nc.sync.dma_start(idx2[:], offs2)
         load_rows(w3_raw[1], w3, 1)
-        load_page(TILE_ORDER[0])
-        load_page(TILE_ORDER[1])
-        load_page(TILE_ORDER[2])
-        load_page(TILE_ORDER[3])
+        load_page(a_t)
+        load_weights(early_a[0], a_t, 1, 0, QUARTER)
+        load_page(b_t)
+        load_weights(early_a[1], a_t, 1, QUARTER, QUARTER)
+        load_weights(early_bc, b_t, 2, 0)
+        load_page(c_t)
+        load_page(d_t)
+        load_weights(late_ad, a_t, 2, HALF)
+        load_weights(early_d, d_t, 1, 0)
+        load_weights(late_bc, b_t, 2, HALF)
         nc.sync.dma_start(idx3[:], offs3)
         nc.sync.dma_start(idx4[:], offs4)
         nc.sync.dma_start(mirrors[:], mirror.rearrange("(p t) -> p t", t=PACK))
         w4_raw = sbuf([P, PACK, N], F32, "w4_raw", "raw0")
         load_rows(w4_raw, w4, 0)
 
-        w1_codes = [sbuf([P, R], U32, "w1_codes%d" % a) for a in range(2)]
-        w1_scales = [sbuf([P, R], U8, "w1_scales%d" % a) for a in range(2)]
-        w3_codes = [sbuf([P, H], U32, "w3_codes%d" % a) for a in range(2)]
-        w3_scales = [sbuf([P, H], U8, "w3_scales%d" % a) for a in range(2)]
-
-        def deal(copy, raw, t0, nt, name, tag):
+        def deal(copy, raw, t0, nt, name, tag=None):
             dealt = sbuf([P, nt, P, PACK], BF16, name, tag)
             copy(
                 dealt[:].rearrange("p t m j -> p m j t"),
@@ -110,33 +137,33 @@ def tile_list_scouting_belief_exchange_kernel(
             )
             return dealt
 
-        def quantise_dealt(dealt, codes, scales, t0, nt):
-            cols = slice(P * t0, P * (t0 + nt))
-            nc.vector.quantize_mx(codes[:, cols].bitcast(FP8X4), scales[:, cols], dealt[:].rearrange("p t m j -> p (t m j)"))
+        def quantise(codes, scales, rounded):
+            nc.vector.quantize_mx(codes.bitcast(FP8X4), scales, rounded)
 
-        for a in range(2):
-            quantise_dealt(deal(nc.vector.tensor_copy, w1_raw[a], 0, PACK, "w1_dealt%d" % a, "wide%d" % a),
-                           w1_codes[a], w1_scales[a], 0, PACK)
+        def flat(dealt):
+            return dealt[:].rearrange("p t m j -> p (t m j)")
 
+        w1_codes = [sbuf([P, R], U32, "w1_codes%d" % a) for a in range(2)]
+        w1_scales = [sbuf([P, R], U8, "w1_scales%d" % a) for a in range(2)]
+        for a, copy in enumerate((nc.scalar.copy, nc.vector.tensor_copy)):
+            quantise(w1_codes[a][:], w1_scales[a][:], flat(deal(copy, w1_raw[a], 0, PACK, "w1_dealt%d" % a, "wide%d" % a)))
 
         v_codes = [sbuf([P, S], U32, "v_codes%d" % a) for a in range(2)]
-        v_scales = sbuf([P, S], U8, "v_scales")
-
-        def entries(tile, j0, n):
-            return tile[:, j0 // PER_COLUMN : (j0 + n) // PER_COLUMN]
 
         def gather_words(a, j0, n):
             nc.vector.tensor_copy(v_codes[a][:, j0 : j0 + n], table[a][:].indirect(entries(idx, j0, n)))
 
-        def times_v(acc, codes, scales, t, a, j0, n, start, stop):
-            cols = slice(P * t, P * (t + 1))
+        def times_v(acc, codes, scales, a, j0, n, start, stop):
             nc.tensor.matmul_mx(
-                acc, lhsT=codes[a][:, cols].bitcast(FP8X4), lhsT_scale=scales[a][:, cols],
-                rhs=v_codes[a][:, j0 : j0 + n].bitcast(FP8X4), rhs_scale=v_scales[4 * a :, j0 : j0 + n],
+                acc, lhsT=codes.bitcast(FP8X4), lhsT_scale=scales,
+                rhs=v_codes[a][:, j0 : j0 + n].bitcast(FP8X4), rhs_scale=v_scales[a][:, j0 : j0 + n],
                 start=start, stop=stop,
             )
 
-        nc.vector.tensor_copy(v_scales[:], table_scales[:].indirect(idx[:]))
+        def w1_times_v(acc, t, a, j0, n, start, stop):
+            cols = slice(P * t, P * (t + 1))
+            times_v(acc, w1_codes[a][:, cols], w1_scales[a][:, cols], a, j0, n, start, stop)
+
         gather_words(0, 0, S)
 
         w2_codes = sbuf([P, 2 * H], U8, "w2_codes")
@@ -150,126 +177,129 @@ def tile_list_scouting_belief_exchange_kernel(
             w2_raw_scales[:].rearrange("p (m t) -> p m t", t=PACK),
         )
 
-        d_codes = sbuf([P, S], U32, "d_codes")
+        d_early_codes = sbuf([P, HALF], U32, "d_early_codes")
         d_scales = sbuf([P, S], U8, "d_scales")
-
-        def quantise_d(rounded, j0, n):
-            nc.vector.quantize_mx(d_codes[:, j0 : j0 + n].bitcast(FP8X4), d_scales[:, j0 : j0 + n],
-                                  rounded[:].rearrange("p j t -> p (j t)"))
 
         def first_half_pass(s, a):
             for t in range(PACK):
-                times_v(banks[s][:, P * t : P * (t + 1)], w1_codes, w1_scales, t, a, P * s, P,
-                        a == 0 and t == 0, a == 1 and t == PACK - 1)
+                w1_times_v(banks[s][:, P * t : P * (t + 1)], t, a, P * s, P, a == 0 and t == 0, a == 1 and t == PACK - 1)
 
         def first_half_tanh(s):
-            bent = sbuf([P, P, PACK], F32, "bent%d" % s, "bent%d" % s)
+            bent = sbuf([P, P, PACK], F32, "bent%d" % s)
             nc.scalar.activation(bent[:], banks[s][:].rearrange("p (t j) -> p j t", t=PACK), ACT.Tanh)
             return bent
 
-        def first_half_gain(rounded, s, bent):
-            nc.vector.tensor_tensor(rounded[:, P * (s % 2) : P * (s % 2 + 1), :], bent[:],
-                                    gains[:].to_broadcast([P, P, PACK]), ALU.mult)
-
-        direct_sb = [sbuf([P, HALF], F32, "direct%d" % i) for i in range(3)]
-        h_sb = [sbuf([P, HALF], F32, "h%d" % i) for i in range(4)]
-        a_t, b_t, c_t, d_t = TILE_ORDER
-        units = [(a_t, 0, 256), (a_t, 256, 256), (b_t, 0, HALF), (c_t, 0, HALF), (d_t, 0, HALF),
-                 (a_t, HALF, HALF), (b_t, HALF, HALF), (c_t, HALF, HALF), (d_t, HALF, HALF)]
+        units = [(t, j0) for j0 in (0, HALF) for t in TILE_ORDER]
+        h_tags = ("h0", "h0", "wgs_early_a1", "h0", "h0", "wgs_early_d", "h1", "gate0")
+        w3_scales = [sbuf([P, H], U8, "w3_scales%d" % a) for a in range(2)]
+        w3_codes = {}
+        d_codes = {0: d_early_codes}
+        h_sb = {}
 
         def make_h(k):
-            t, j0, n = units[k]
+            t, j0 = units[k]
+            n = HALF
             direct_bank, deep_bank = banks[4 + 2 * (k % 2)], banks[5 + 2 * (k % 2)]
-            for a in range(2):
-                times_v(direct_bank[:, :n], w3_codes, w3_scales, t, a, j0, n, a == 0, a == 1)
-            nc.scalar.copy(direct_sb[k % 3][:, :n], direct_bank[:, :n])
             nc.tensor.matmul_mx(
                 deep_bank[:, :n], lhsT=w2_codes[:, 2 * P * t : 2 * P * (t + 1)].bitcast(FP4X4),
                 lhsT_scale=w2_dealt_scales[:, P * t : P * (t + 1)],
-                rhs=d_codes[:, j0 : j0 + n].bitcast(FP8X4), rhs_scale=d_scales[:, j0 : j0 + n], start=True, stop=True,
+                rhs=d_codes[j0 // HALF][:, j0 % HALF : j0 % HALF + n].bitcast(FP8X4),
+                rhs_scale=d_scales[:, j0 : j0 + n], start=True, stop=True,
             )
-            nc.vector.tensor_tensor(h_sb[k % 4][:, :n], deep_bank[:, :n], direct_sb[k % 3][:, :n], ALU.max)
+            deep = sbuf([P, n], F32, "deep_unit%d" % k, "deep%d" % (k % 2))
+            nc.scalar.copy(deep[:], deep_bank[:, :n])
+            for a in range(2):
+                times_v(direct_bank[:, :n], w3_codes[a, t], w3_scales[a][:, P * t : P * (t + 1)], a, j0, n, a == 0, a == 1)
+            h_sb[k] = sbuf([P, n], F32, "h_unit%d" % k, h_tags[k])
+            nc.vector.tensor_tensor(h_sb[k][:], direct_bank[:, :n], deep[:], ALU.max)
 
         def put_h(k):
-            t, j0, n = units[k]
-            nc.vector.tensor_tensor(page[t][:].indirect(entries(idx2, j0, n)), h_sb[k % 4][:, :n],
-                                    weights[t][:, j0 : j0 + n], ALU.mult)
+            t, j0 = units[k]
+            factor = early_weights[t] if j0 < HALF else late_weights[t]
+            nc.vector.tensor_tensor(page[t][:].indirect(entries(idx2, j0, HALF)), h_sb[k][:], factor, ALU.mult)
+
+        def put_first(c):
+            nc.vector.tensor_tensor(page[a_t][:].indirect(entries(idx2, QUARTER * c, QUARTER)),
+                                    h_sb[0][:, QUARTER * c : QUARTER * (c + 1)], early_a[c][:, 0, :], ALU.mult)
 
         for s in range(4):
             first_half_pass(s, 0)
-        gather_words(1, 0, 256)
-        first_half_pass(0, 1)
-        first_half_pass(1, 1)
-        bent = [first_half_tanh(0), first_half_tanh(1)]
-        gather_words(1, 256, 256)
-        first_half_pass(2, 1)
-        first_half_pass(3, 1)
-        bent = bent + [first_half_tanh(2), first_half_tanh(3)]
-        d_rounded = [sbuf([P, 256, PACK], BF16, "d_rounded%d" % c) for c in range(2)]
-        first_half_gain(d_rounded[0], 0, bent[0])
-        first_half_gain(d_rounded[0], 1, bent[1])
-        low0 = deal(nc.vector.tensor_copy, w3_raw[0], 0, 2, "w3_low0", "narrow0")
-        quantise_d(d_rounded[0], 0, 256)
-        first_half_gain(d_rounded[1], 2, bent[2])
-        quantise_dealt(low0, w3_codes[0], w3_scales[0], 0, 2)
-        high0 = deal(nc.scalar.copy, w3_raw[0], 2, 2, "w3_high0", "narrow2")
-        first_half_gain(d_rounded[1], 3, bent[3])
-        low1 = deal(nc.vector.tensor_copy, w3_raw[1], 0, 2, "w3_low1", "narrow1")
-        quantise_d(d_rounded[1], 256, 256)
-        quantise_dealt(low1, w3_codes[1], w3_scales[1], 0, 2)
-        high1 = deal(nc.scalar.copy, w3_raw[1], 2, 2, "w3_high1", "narrow3")
+        bent = []
+        for c in range(2):
+            gather_words(1, QUARTER * c, QUARTER)
+            for s in (2 * c, 2 * c + 1):
+                first_half_pass(s, 1)
+                bent.append(first_half_tanh(s))
         gather_words(1, HALF, HALF)
+        d_early = sbuf([P, HALF, PACK], BF16, "d_early")
+        for s in range(4):
+            nc.vector.tensor_tensor(d_early[:, P * s : P * (s + 1), :], bent[s][:],
+                                    gains[:].to_broadcast([P, P, PACK]), ALU.mult)
+        w3_first_codes = sbuf([P, 2, P], U32, "w3_first_codes")
+        first = [deal(nc.vector.tensor_copy, w3_raw[0], a_t, 1, "w3_first0")]
+        quantise(d_early_codes[:], d_scales[:, :HALF], d_early[:].rearrange("p j t -> p (j t)"))
+        first.append(deal(nc.vector.tensor_copy, w3_raw[1], a_t, 1, "w3_first1"))
+        for a in range(2):
+            quantise(w3_first_codes[:, a, :], w3_scales[a][:, :P], flat(first[a]))
+            w3_codes[a, a_t] = w3_first_codes[:, a, :]
         make_h(0)
+        rest = [deal(nc.scalar.copy, w3_raw[a], 1, 3, "w3_rest%d" % a) for a in range(2)]
+        put_first(0)
+        w3_rest_codes = sbuf([P, 2, 3 * P], U32, "w3_rest_codes", "wgs_early_a0")
+        for a in range(2):
+            quantise(w3_rest_codes[:, a, :], w3_scales[a][:, P:], flat(rest[a]))
+            for t in range(1, PACK):
+                w3_codes[a, t] = w3_rest_codes[:, a, P * (t - 1) : P * t]
+        put_first(1)
         make_h(1)
-        quantise_dealt(high0, w3_codes[0], w3_scales[0], 2, 2)
-        put_h(0)
-        quantise_dealt(high1, w3_codes[1], w3_scales[1], 2, 2)
-        put_h(1)
         make_h(2)
+        put_h(1)
         make_h(3)
 
         scaled = sbuf([P, PACK, HALF], BF16, "d_scaled", "wide2")
         for t in range(PACK):
             for a in range(2):
-                times_v(banks[t][:], w1_codes, w1_scales, t, a, HALF, HALF, a == 0, a == 1)
-            late = sbuf([P, HALF], F32, "late%d" % t, "bent%d" % t)
+                w1_times_v(banks[t][:], t, a, HALF, HALF, a == 0, a == 1)
+            late = sbuf([P, HALF], F32, "late%d" % t, ("w3_first1", "w3_rest1")[t % 2])
             nc.scalar.activation(late[:], banks[t][:], ACT.Tanh)
             nc.scalar.activation(scaled[:, t, :], late[:], ACT.Copy, scale=gains[:, 0, t : t + 1])
         d_late = sbuf([P, HALF, PACK], BF16, "d_late")
-        put_h(2)
-        make_h(4)
         nc.scalar.copy(d_late[:].rearrange("p (c i) t -> p c t i", i=4), scaled[:].rearrange("p t (c i) -> p c t i", i=4))
+        put_h(2)
+        d_codes[1] = sbuf([P, HALF], U32, "d_late_codes", "wgs_early_bc")
+        quantise(d_codes[1][:], d_scales[:, HALF:], d_late[:].rearrange("p j t -> p (j t)"))
         put_h(3)
-        quantise_d(d_late, HALF, HALF)
+        make_h(4)
         make_h(5)
         put_h(4)
         make_h(6)
         put_h(5)
-        make_h(7)
-        put_h(6)
 
         w4_rounded = sbuf([P, N, PACK], BF16, "w4_rounded", "wide0")
-        w4_codes = sbuf([P, N], U32, "w4_codes")
         w4_scales = sbuf([P, N], U8, "w4_scales")
 
         one_side = [sbuf([P, PAIRS], F32, "one_side%d" % i) for i in range(2)]
         other_side = [sbuf([P, PAIRS], F32, "other_side%d" % i) for i in range(2)]
-        gate = [sbuf([P, PAIRS], F32, "gate%d" % i) for i in range(2)]
+        gate = {}
 
         def fetch(i):
             t = TILE_ORDER[i]
             nc.vector.tensor_copy(other_side[i % 2][:], page[t][:].indirect(idx4[:]))
             nc.vector.tensor_copy(one_side[i % 2][:], page[t][:].indirect(idx3[:]))
-            nc.scalar.activation(gate[i % 2][:], other_side[i % 2][:], ACT.Tanh, scale=mirrors[:, t : t + 1])
+
+        def make_gate(i):
+            t = TILE_ORDER[i]
+            gate[i] = sbuf([P, PAIRS], F32, "gate_tile%d" % i, "gate%d" % (i % 2))
+            nc.scalar.activation(gate[i][:], other_side[i % 2][:], ACT.Tanh, scale=mirrors[:, t : t + 1])
 
         def put_sum(i):
             nc.vector.tensor_tensor(page[TILE_ORDER[i]][:].indirect(idx4[:]), one_side[i % 2][:], other_side[i % 2][:], ALU.add)
 
         def put_gated(i):
-            nc.vector.tensor_tensor(page[TILE_ORDER[i]][:].indirect(idx3[:]), one_side[i % 2][:], gate[i % 2][:], ALU.mult)
+            nc.vector.tensor_tensor(page[TILE_ORDER[i]][:].indirect(idx3[:]), one_side[i % 2][:], gate[i][:], ALU.mult)
 
         starts = [sum(OUT_WIDTHS[:c]) for c in range(len(OUT_WIDTHS))]
-        tags = ("narrow0", "narrow1", "wide1", "wide2", "d_late")
+        tags = ("bent0", "bent1", "wide1", "wide2", "d_late")
         rounded = [sbuf([P, w, PACK], BF16, "page_rounded%d" % c, tags[c]) for c, w in enumerate(OUT_WIDTHS)]
 
         def round_page(copy, t, c):
@@ -280,24 +310,29 @@ def tile_list_scouting_belief_exchange_kernel(
                 round_page(nc.scalar.copy, TILE_ORDER[i], c)
 
         fetch(0)
-        make_h(8)
+        make_gate(0)
         nc.scalar.copy(w4_rounded[:].rearrange("p (c i) j -> p c j i", i=4), w4_raw[:].rearrange("p j (c i) -> p c j i", i=4))
-        put_h(7)
+        put_h(6)
         put_sum(0)
         fetch(1)
+        make_gate(1)
         put_gated(0)
-        round_early(0)
         put_sum(1)
+        make_h(7)
+        round_early(0)
         fetch(2)
         put_gated(1)
+        put_h(7)
+        make_gate(2)
         round_early(1)
-        put_h(8)
         put_sum(2)
         fetch(3)
+        make_gate(3)
         put_gated(2)
         round_early(2)
         put_sum(3)
-        nc.vector.quantize_mx(w4_codes[:].bitcast(FP8X4), w4_scales[:], w4_rounded[:].rearrange("p n j -> p (n j)"))
+        w4_codes = sbuf([P, N], U32, "w4_codes", "one_side0")
+        quantise(w4_codes[:], w4_scales[:], w4_rounded[:].rearrange("p n j -> p (n j)"))
         put_gated(3)
 
         page_codes = [sbuf([P, w], U32, "page_codes%d" % c) for c, w in enumerate(OUT_WIDTHS)]
@@ -306,10 +341,13 @@ def tile_list_scouting_belief_exchange_kernel(
         first_bank = (0, 2, 4, 0, 4)
         out_rows = out.rearrange("(g p) c -> p g c", p=P)
 
+        def quantise_page(c):
+            quantise(page_codes[c][:], page_scales[c][:], rounded[c][:].rearrange("p c t -> p (c t)"))
+
         def finish(c):
             w = OUT_WIDTHS[c]
             per_bank = BANK // w
-            nc.vector.quantize_mx(page_codes[c][:].bitcast(FP8X4), page_scales[c][:], rounded[c][:].rearrange("p c t -> p (c t)"))
+            per_store = max(per_bank, 1 if c == len(OUT_WIDTHS) - 1 else 2)
             stage = sbuf([P, PACK, w], F32, "stage%d" % c, stage_tags[c])
             for g in range(PACK):
                 bank = banks[first_bank[c] + g // per_bank]
@@ -319,14 +357,16 @@ def tile_list_scouting_belief_exchange_kernel(
                     rhs=page_codes[c][:].bitcast(FP8X4), rhs_scale=page_scales[c][:], start=True, stop=True,
                 )
                 if g % per_bank == per_bank - 1:
-                    copy = nc.vector.tensor_copy if (per_bank == 1 and g == PACK - 1) else nc.scalar.copy
-                    g0 = g - per_bank + 1
-                    copy(stage[:, g0 : g + 1, :].rearrange("p g c -> p (g c)"), bank[:])
-                if g % 2 == 1:
-                    nc.sync.dma_start(out_rows[:, g - 1 : g + 1, starts[c] : starts[c] + w], stage[:, g - 1 : g + 1, :])
+                    copy = nc.vector.tensor_copy if (c >= len(OUT_WIDTHS) - 2 and g >= 2) else nc.scalar.copy
+                    copy(stage[:, g - per_bank + 1 : g + 1, :].rearrange("p g c -> p (g c)"), bank[:])
+                if g % per_store == per_store - 1:
+                    rows = slice(g - per_store + 1, g + 1)
+                    nc.sync.dma_start(out_rows[:, rows, starts[c] : starts[c] + w], stage[:, rows, :])
 
         round_page(nc.vector.tensor_copy, d_t, 0)
         for c in range(len(OUT_WIDTHS)):
             if c + 1 < len(OUT_WIDTHS):
                 round_page(nc.vector.tensor_copy, d_t, c + 1)
+            quantise_page(c)
+        for c in range(len(OUT_WIDTHS)):
             finish(c)

from contextlib import ExitStack

import concourse.mybir as mybir

K, R, H, N, T, S, T2, PAIRS = 1024, 512, 512, 512, 4096, 1024, 2048, 512
FLOPS = 2 * S * (K * R + R * H + K * H) + 2 * H * N * T2

F32 = mybir.dt.float32
BF16 = mybir.dt.bfloat16
I32 = mybir.dt.int32
U32 = mybir.dt.uint32
U16 = mybir.dt.uint16
U8 = mybir.dt.uint8
FP8X4 = mybir.dt.float8_e4m3fn_x4
FP4X4 = mybir.dt.float4_e2m1fn_x4
ALU = mybir.AluOpType
ACT = mybir.ActivationFunctionType

P = 128
PACK = 4
BANK = 512
HALF = S // 2
QUARTER = S // 4
PER_COLUMN = 16
TILE_ORDER = (0, 2, 3, 1)
OUT_WIDTHS = (256, 256, 512, 512, 512)


def tile_list_scouting_belief_exchange_kernel(
    tc, tab_words, tab_scales, offs, w1, gain, w2_words, w2_scales, w3, page0, wgs, offs2, offs3, offs4, mirror, w4, out
):
    nc = tc.nc
    with ExitStack() as ctx:
        sb = ctx.enter_context(tc.tile_pool(name="sb", bufs=1))
        ps = ctx.enter_context(tc.psum_pool(name="ps", bufs=1))

        def sbuf(shape, dtype, name, tag=None):
            return sb.tile(shape, dtype, name=name, tag=tag or name, align_bytes=64)

        banks = [ps.tile([P, BANK], F32, name="bank%d" % i) for i in range(8)]

        idx = sbuf([P, S // PER_COLUMN], U16, "idx")
        idx2 = sbuf([P, S // PER_COLUMN], U16, "idx2")
        idx3 = sbuf([P, PAIRS // PER_COLUMN], U16, "idx3")
        idx4 = sbuf([P, PAIRS // PER_COLUMN], U16, "idx4")
        table = [sbuf([P, T], U32, "table%d" % a) for a in range(2)]
        table_scales = sbuf([P, T], U8, "table_scales")
        w1_raw = [sbuf([P, PACK, R], F32, "w1_raw%d" % a, "raw%d" % a) for a in range(2)]
        w3_raw = [sbuf([P, PACK, H], F32, "w3_raw%d" % a, "raw%d" % (2 + a)) for a in range(2)]
        w2_raw = sbuf([P, 2 * H], U8, "w2_raw")
        w2_raw_scales = sbuf([P, H], U8, "w2_raw_scales")
        gains = sbuf([P, 1, PACK], F32, "gains")
        mirrors = sbuf([P, PACK], F32, "mirrors")
        page = [sbuf([P, T2], F32, "page%d" % t) for t in range(PACK)]
        a_t, b_t, c_t, d_t = TILE_ORDER
        early_a = [sbuf([P, 1, QUARTER], F32, "wgs_early_a%d" % c) for c in range(2)]
        early_bc = sbuf([P, 2, HALF], F32, "wgs_early_bc")
        early_d = sbuf([P, 1, HALF], F32, "wgs_early_d")
        late_ad = sbuf([P, 2, HALF], F32, "wgs_late_ad")
        late_bc = sbuf([P, 2, HALF], F32, "wgs_late_bc")
        late_weights = {a_t: late_ad[:, 0, :], d_t: late_ad[:, 1, :], b_t: late_bc[:, 0, :], c_t: late_bc[:, 1, :]}
        early_weights = {b_t: early_bc[:, 0, :], c_t: early_bc[:, 1, :], d_t: early_d[:, 0, :]}

        nc.gpsimd.memset(w2_raw_scales[:].bitcast(I32), 0)
        nc.gpsimd.memset(table_scales[32:64, :].bitcast(I32), 0)
        nc.vector.memset(table_scales[64:, :].bitcast(I32), 0)
        v_scales = [sbuf([P, S], U8, "v_scales%d" % a) for a in range(2)]
        for a in range(2):
            nc.vector.memset(v_scales[a][:].bitcast(I32), 0)

        def load_rows(tile, w, a):
            nc.sync.dma_start(tile[:], w[512 * a : 512 * (a + 1), :].rearrange("(p j) c -> p j c", j=PACK))

        def load_table(a):
            nc.sync.dma_start(table[a][:].bitcast(I32), tab_words[a].rearrange("p t i -> p (t i)").bitcast(I32))

        def load_page(t):
            nc.sync.dma_start(page[t][:], page0.rearrange("(p t) c -> t p c", t=PACK)[t])

        def load_weights(tile, t0, nt, j0, n=HALF):
            rows = wgs.rearrange("(u t) j -> u t j", t=PACK)[:, t0 : t0 + nt, j0 : j0 + n]
            for q in (0, 2, 1, 3):
                nc.sync.dma_start(tile[32 * q : 32 * (q + 1), :, :], rows)

        def entries(tile, j0, n):
            return tile[:, j0 // PER_COLUMN : (j0 + n) // PER_COLUMN]

        picked_scales = sbuf([P, S], U8, "picked_scales")

        def place_scales(a, r):
            nc.sync.dma_start(
                v_scales[a][r:P:32, :].bitcast(I32), picked_scales[16 * a + r : 16 * (a + 1) : 4, :].bitcast(I32)
            )

        nc.sync.dma_start(table_scales[:32, :].bitcast(I32), tab_scales.rearrange("a q t -> (a q) t").bitcast(I32))
        nc.sync.dma_start(idx[:], offs)
        load_rows(w1_raw[0], w1, 0)
        nc.sync.dma_start(w2_raw[:].bitcast(I32), w2_words[0].bitcast(I32))
        for q in range(4):
            nc.sync.dma_start(
                w2_raw_scales[32 * q : 32 * q + 4, :].bitcast(I32), w2_scales[0, 4 * q : 4 * q + 4, :].bitcast(I32)
            )
        load_rows(w1_raw[1], w1, 1)
        load_table(0)
        nc.vector.tensor_copy(picked_scales[:], table_scales[:].indirect(idx[:]))
        scale_rows = [(a, r) for a in range(2) for r in range(4)]
        for a, r in scale_rows[:6]:
            place_scales(a, r)
        load_table(1)
        for a, r in scale_rows[6:]:
            place_scales(a, r)
        load_rows(w3_raw[0], w3, 0)
        nc.sync.dma_start(gains[:, 0, :], gain.rearrange("(p t) -> p t", t=PACK))
        nc.sync.dma_start(idx2[:], offs2)
        load_rows(w3_raw[1], w3, 1)
        load_page(a_t)
        load_weights(early_a[0], a_t, 1, 0, QUARTER)
        load_page(b_t)
        load_weights(early_a[1], a_t, 1, QUARTER, QUARTER)
        load_weights(early_bc, b_t, 2, 0)
        load_page(c_t)
        load_page(d_t)
        load_weights(late_ad, a_t, 2, HALF)
        load_weights(early_d, d_t, 1, 0)
        load_weights(late_bc, b_t, 2, HALF)
        nc.sync.dma_start(idx3[:], offs3)
        nc.sync.dma_start(idx4[:], offs4)
        nc.sync.dma_start(mirrors[:], mirror.rearrange("(p t) -> p t", t=PACK))
        w4_raw = sbuf([P, PACK, N], F32, "w4_raw", "raw0")
        load_rows(w4_raw, w4, 0)

        def deal(copy, raw, t0, nt, name, tag=None):
            dealt = sbuf([P, nt, P, PACK], BF16, name, tag)
            copy(
                dealt[:].rearrange("p t m j -> p m j t"),
                raw[:].rearrange("p j (m t) -> p m j t", t=PACK)[:, :, :, t0 : t0 + nt],
            )
            return dealt

        def quantise(codes, scales, rounded):
            nc.vector.quantize_mx(codes.bitcast(FP8X4), scales, rounded)

        def flat(dealt):
            return dealt[:].rearrange("p t m j -> p (t m j)")

        w1_codes = [sbuf([P, R], U32, "w1_codes%d" % a) for a in range(2)]
        w1_scales = [sbuf([P, R], U8, "w1_scales%d" % a) for a in range(2)]
        for a, copy in enumerate((nc.scalar.copy, nc.vector.tensor_copy)):
            quantise(w1_codes[a][:], w1_scales[a][:], flat(deal(copy, w1_raw[a], 0, PACK, "w1_dealt%d" % a, "wide%d" % a)))

        v_codes = [sbuf([P, S], U32, "v_codes%d" % a) for a in range(2)]

        def gather_words(a, j0, n):
            nc.vector.tensor_copy(v_codes[a][:, j0 : j0 + n], table[a][:].indirect(entries(idx, j0, n)))

        def times_v(acc, codes, scales, a, j0, n, start, stop):
            nc.tensor.matmul_mx(
                acc, lhsT=codes.bitcast(FP8X4), lhsT_scale=scales,
                rhs=v_codes[a][:, j0 : j0 + n].bitcast(FP8X4), rhs_scale=v_scales[a][:, j0 : j0 + n],
                start=start, stop=stop,
            )

        def w1_times_v(acc, t, a, j0, n, start, stop):
            cols = slice(P * t, P * (t + 1))
            times_v(acc, w1_codes[a][:, cols], w1_scales[a][:, cols], a, j0, n, start, stop)

        gather_words(0, 0, S)

        w2_codes = sbuf([P, 2 * H], U8, "w2_codes")
        w2_dealt_scales = sbuf([P, H], U8, "w2_dealt_scales")
        nc.vector.tensor_copy(
            w2_codes[:].rearrange("p (t m b) -> p m t b", t=PACK, b=2),
            w2_raw[:].rearrange("p (m t b) -> p m t b", t=PACK, b=2),
        )
        nc.vector.tensor_copy(
            w2_dealt_scales[:].rearrange("p (t m) -> p m t", t=PACK),
            w2_raw_scales[:].rearrange("p (m t) -> p m t", t=PACK),
        )

        d_early_codes = sbuf([P, HALF], U32, "d_early_codes")
        d_scales = sbuf([P, S], U8, "d_scales")

        def first_half_pass(s, a):
            for t in range(PACK):
                w1_times_v(banks[s][:, P * t : P * (t + 1)], t, a, P * s, P, a == 0 and t == 0, a == 1 and t == PACK - 1)

        def first_half_tanh(s):
            bent = sbuf([P, P, PACK], F32, "bent%d" % s)
            nc.scalar.activation(bent[:], banks[s][:].rearrange("p (t j) -> p j t", t=PACK), ACT.Tanh)
            return bent

        units = [(t, j0) for j0 in (0, HALF) for t in TILE_ORDER]
        h_tags = ("h0", "h0", "wgs_early_a1", "h0", "h0", "wgs_early_d", "h1", "gate0")
        w3_scales = [sbuf([P, H], U8, "w3_scales%d" % a) for a in range(2)]
        w3_codes = {}
        d_codes = {0: d_early_codes}
        h_sb = {}

        def make_h(k):
            t, j0 = units[k]
            n = HALF
            direct_bank, deep_bank = banks[4 + 2 * (k % 2)], banks[5 + 2 * (k % 2)]
            nc.tensor.matmul_mx(
                deep_bank[:, :n], lhsT=w2_codes[:, 2 * P * t : 2 * P * (t + 1)].bitcast(FP4X4),
                lhsT_scale=w2_dealt_scales[:, P * t : P * (t + 1)],
                rhs=d_codes[j0 // HALF][:, j0 % HALF : j0 % HALF + n].bitcast(FP8X4),
                rhs_scale=d_scales[:, j0 : j0 + n], start=True, stop=True,
            )
            deep = sbuf([P, n], F32, "deep_unit%d" % k, "deep%d" % (k % 2))
            nc.scalar.copy(deep[:], deep_bank[:, :n])
            for a in range(2):
                times_v(direct_bank[:, :n], w3_codes[a, t], w3_scales[a][:, P * t : P * (t + 1)], a, j0, n, a == 0, a == 1)
            h_sb[k] = sbuf([P, n], F32, "h_unit%d" % k, h_tags[k])
            nc.vector.tensor_tensor(h_sb[k][:], direct_bank[:, :n], deep[:], ALU.max)

        def put_h(k):
            t, j0 = units[k]
            factor = early_weights[t] if j0 < HALF else late_weights[t]
            nc.vector.tensor_tensor(page[t][:].indirect(entries(idx2, j0, HALF)), h_sb[k][:], factor, ALU.mult)

        def put_first(c):
            nc.vector.tensor_tensor(page[a_t][:].indirect(entries(idx2, QUARTER * c, QUARTER)),
                                    h_sb[0][:, QUARTER * c : QUARTER * (c + 1)], early_a[c][:, 0, :], ALU.mult)

        for s in range(4):
            first_half_pass(s, 0)
        bent = []
        for c in range(2):
            gather_words(1, QUARTER * c, QUARTER)
            for s in (2 * c, 2 * c + 1):
                first_half_pass(s, 1)
                bent.append(first_half_tanh(s))
        gather_words(1, HALF, HALF)
        d_early = sbuf([P, HALF, PACK], BF16, "d_early")
        for s in range(4):
            nc.vector.tensor_tensor(d_early[:, P * s : P * (s + 1), :], bent[s][:],
                                    gains[:].to_broadcast([P, P, PACK]), ALU.mult)
        w3_first_codes = sbuf([P, 2, P], U32, "w3_first_codes")
        first = [deal(nc.vector.tensor_copy, w3_raw[0], a_t, 1, "w3_first0")]
        quantise(d_early_codes[:], d_scales[:, :HALF], d_early[:].rearrange("p j t -> p (j t)"))
        first.append(deal(nc.vector.tensor_copy, w3_raw[1], a_t, 1, "w3_first1"))
        for a in range(2):
            quantise(w3_first_codes[:, a, :], w3_scales[a][:, :P], flat(first[a]))
            w3_codes[a, a_t] = w3_first_codes[:, a, :]
        make_h(0)
        rest = [deal(nc.scalar.copy, w3_raw[a], 1, 3, "w3_rest%d" % a) for a in range(2)]
        put_first(0)
        w3_rest_codes = sbuf([P, 2, 3 * P], U32, "w3_rest_codes", "wgs_early_a0")
        for a in range(2):
            quantise(w3_rest_codes[:, a, :], w3_scales[a][:, P:], flat(rest[a]))
            for t in range(1, PACK):
                w3_codes[a, t] = w3_rest_codes[:, a, P * (t - 1) : P * t]
        put_first(1)
        make_h(1)
        make_h(2)
        put_h(1)
        make_h(3)

        scaled = sbuf([P, PACK, HALF], BF16, "d_scaled", "wide2")
        for t in range(PACK):
            for a in range(2):
                w1_times_v(banks[t][:], t, a, HALF, HALF, a == 0, a == 1)
            late = sbuf([P, HALF], F32, "late%d" % t, ("w3_first1", "w3_rest1")[t % 2])
            nc.scalar.activation(late[:], banks[t][:], ACT.Tanh)
            nc.scalar.activation(scaled[:, t, :], late[:], ACT.Copy, scale=gains[:, 0, t : t + 1])
        d_late = sbuf([P, HALF, PACK], BF16, "d_late")
        nc.scalar.copy(d_late[:].rearrange("p (c i) t -> p c t i", i=4), scaled[:].rearrange("p t (c i) -> p c t i", i=4))
        put_h(2)
        d_codes[1] = sbuf([P, HALF], U32, "d_late_codes", "wgs_early_bc")
        quantise(d_codes[1][:], d_scales[:, HALF:], d_late[:].rearrange("p j t -> p (j t)"))
        put_h(3)
        make_h(4)
        make_h(5)
        put_h(4)
        make_h(6)
        put_h(5)

        w4_rounded = sbuf([P, N, PACK], BF16, "w4_rounded", "wide0")
        w4_scales = sbuf([P, N], U8, "w4_scales")

        one_side = [sbuf([P, PAIRS], F32, "one_side%d" % i) for i in range(2)]
        other_side = [sbuf([P, PAIRS], F32, "other_side%d" % i) for i in range(2)]
        gate = {}

        def fetch(i):
            t = TILE_ORDER[i]
            nc.vector.tensor_copy(other_side[i % 2][:], page[t][:].indirect(idx4[:]))
            nc.vector.tensor_copy(one_side[i % 2][:], page[t][:].indirect(idx3[:]))

        def make_gate(i):
            t = TILE_ORDER[i]
            gate[i] = sbuf([P, PAIRS], F32, "gate_tile%d" % i, "gate%d" % (i % 2))
            nc.scalar.activation(gate[i][:], other_side[i % 2][:], ACT.Tanh, scale=mirrors[:, t : t + 1])

        def put_sum(i):
            nc.vector.tensor_tensor(page[TILE_ORDER[i]][:].indirect(idx4[:]), one_side[i % 2][:], other_side[i % 2][:], ALU.add)

        def put_gated(i):
            nc.vector.tensor_tensor(page[TILE_ORDER[i]][:].indirect(idx3[:]), one_side[i % 2][:], gate[i][:], ALU.mult)

        starts = [sum(OUT_WIDTHS[:c]) for c in range(len(OUT_WIDTHS))]
        tags = ("bent0", "bent1", "wide1", "wide2", "d_late")
        rounded = [sbuf([P, w, PACK], BF16, "page_rounded%d" % c, tags[c]) for c, w in enumerate(OUT_WIDTHS)]

        def round_page(copy, t, c):
            copy(rounded[c][:, :, t], page[t][:, starts[c] : starts[c] + OUT_WIDTHS[c]])

        def round_early(i):
            for c in range(len(OUT_WIDTHS)):
                round_page(nc.scalar.copy, TILE_ORDER[i], c)

        fetch(0)
        make_gate(0)
        nc.scalar.copy(w4_rounded[:].rearrange("p (c i) j -> p c j i", i=4), w4_raw[:].rearrange("p j (c i) -> p c j i", i=4))
        put_h(6)
        put_sum(0)
        fetch(1)
        make_gate(1)
        put_gated(0)
        put_sum(1)
        make_h(7)
        round_early(0)
        fetch(2)
        put_gated(1)
        put_h(7)
        make_gate(2)
        round_early(1)
        put_sum(2)
        fetch(3)
        make_gate(3)
        put_gated(2)
        round_early(2)
        put_sum(3)
        w4_codes = sbuf([P, N], U32, "w4_codes", "one_side0")
        quantise(w4_codes[:], w4_scales[:], w4_rounded[:].rearrange("p n j -> p (n j)"))
        put_gated(3)

        page_codes = [sbuf([P, w], U32, "page_codes%d" % c) for c, w in enumerate(OUT_WIDTHS)]
        page_scales = [sbuf([P, w], U8, "page_scales%d" % c) for c, w in enumerate(OUT_WIDTHS)]
        stage_tags = ("stage", "raw1", "raw2", "raw3", "raw0")
        first_bank = (0, 2, 4, 0, 4)
        out_rows = out.rearrange("(g p) c -> p g c", p=P)

        def quantise_page(c):
            quantise(page_codes[c][:], page_scales[c][:], rounded[c][:].rearrange("p c t -> p (c t)"))

        def finish(c):
            w = OUT_WIDTHS[c]
            per_bank = BANK // w
            per_store = max(per_bank, 1 if c == len(OUT_WIDTHS) - 1 else 2)
            stage = sbuf([P, PACK, w], F32, "stage%d" % c, stage_tags[c])
            for g in range(PACK):
                bank = banks[first_bank[c] + g // per_bank]
                nc.tensor.matmul_mx(
                    bank[:, w * (g % per_bank) : w * (g % per_bank + 1)],
                    lhsT=w4_codes[:, P * g : P * (g + 1)].bitcast(FP8X4), lhsT_scale=w4_scales[:, P * g : P * (g + 1)],
                    rhs=page_codes[c][:].bitcast(FP8X4), rhs_scale=page_scales[c][:], start=True, stop=True,
                )
                if g % per_bank == per_bank - 1:
                    copy = nc.vector.tensor_copy if (c >= len(OUT_WIDTHS) - 2 and g >= 2) else nc.scalar.copy
                    copy(stage[:, g - per_bank + 1 : g + 1, :].rearrange("p g c -> p (g c)"), bank[:])
                if g % per_store == per_store - 1:
                    rows = slice(g - per_store + 1, g + 1)
                    nc.sync.dma_start(out_rows[:, rows, starts[c] : starts[c] + w], stage[:, rows, :])

        round_page(nc.vector.tensor_copy, d_t, 0)
        for c in range(len(OUT_WIDTHS)):
            if c + 1 < len(OUT_WIDTHS):
                round_page(nc.vector.tensor_copy, d_t, c + 1)
            quantise_page(c)
        for c in range(len(OUT_WIDTHS)):
            finish(c)
